import numpy as np, ml_dtypes
CORES = [21,29,37,45,53,61,69,77,85]
N = 9
import mx_ref
NC, G = 512, 4
C = np.float32(0.047)
BF = ml_dtypes.bfloat16
def cut(t, i, w=512):
    return t[:, w * i:w * i + w]
def tile(rs):
    return np.stack(rs, axis=2).reshape(128, -1).astype(BF)
def act(Z):
    return [np.maximum(z, 0) * C for z in Z]
def setup_inputs(rng):
    def f(*shape):
        return mx_ref.flush((rng.standard_normal(shape, dtype=np.float32) * np.exp2(rng.integers(-2, 3, shape[:-1] + (1,)))).astype(BF))
    return {"x": f(N, 128, 4 * NC), "res": f(N, 128, 4 * NC), "w1": f(N, 128, 512), "w2": f(N, 128, 2 * 512)}
def setup_inputs_blocks(rng):
    d = setup_inputs(rng)
    for k in ("x", "w1", "w2", "res"): d[k] = mx_ref.spread(d[k], rng, 4)
    return d
def setup_inputs_wide(rng):
    d = setup_inputs(rng)
    for k in ("x", "w1", "w2", "res"): d[k] = mx_ref.flush((d[k].astype(np.float32) * np.exp2(rng.integers(-6, 7, (N, 1, 1))).astype(np.float32)).astype(BF))
    return d
def reference(x, res, w1, w2):
    W = [mx_ref.quantize(w1[j]) for j in range(N)]; H = []
    for r in range(N):
        X = mx_ref.quantize(x[r]); e = res[r].astype(np.float32)
        R = act([mx_ref.matmul(W[(r + i) % N], X) for i in range(G)])
        H.append(mx_ref.quantize(tile([R[b] + e[:, b::4] for b in range(4)])))
    y = np.zeros((N, 128, NC), np.float32)
    for r in range(N):
        y[r] = mx_ref.matmul(mx_ref.quantize(cut(w2[r], 0)), H[r]) + mx_ref.matmul(mx_ref.quantize(cut(w2[r], 1)), H[(r + 1) % N])
    return {"y": y}

@@ -1,0 +1,219 @@
+from concourse.bass import DstId, RemoteDMATransfer
+from concourse.mybir import dt, AluOpType, ActivationFunctionType
+
+N = 9
+SIM = 96
+NC = 512
+WC = 128
+G = 4
+HC = NC // 2
+CF = 0.047
+BANK = 512
+NP = 6
+
+_Q, _U = "float8_e4m3fn_x4", "uint8"
+SCRATCH = {
+    "w1b": ("sbuf", [128, 4 * WC], "bfloat16"), "w1q": ("sbuf", [128, WC], _Q), "w1s": ("sbuf", [128, WC], _U),
+    "xb": ("sbuf", [128, 4 * NC], "bfloat16"), "xq": ("sbuf", [128, NC], _Q), "xs": ("sbuf", [128, NC], _U),
+    "w2b": ("sbuf", [128, 8 * WC], "bfloat16"), "w2q": ("sbuf", [128, 2 * WC], _Q), "w2s": ("sbuf", [128, 2 * WC], _U),
+    "rsb": ("sbuf", [128, 4 * NC], "bfloat16"),
+    "ac": ("sbuf", [128, G * NC], "float32"),
+    "hb": ("sbuf", [128, 4 * NC], "bfloat16"), "hq": ("sbuf", [128, NC], _Q), "hs": ("sbuf", [128, NC], _U),
+    "wiq": ("sbuf", [128, 3 * WC], _Q), "wis": ("sbuf", [128, 3 * WC], _U),
+    "hiq": ("sbuf", [128, NC], _Q), "his": ("sbuf", [128, NC], _U),
+    "rwq": ("sbuf", [128, WC], _Q), "rws": ("sbuf", [128, WC], _U),
+    "rhq": ("sbuf", [128, NC], _Q), "rhs": ("sbuf", [128, NC], _U),
+    "yb": ("sbuf", [128, NC], "float32"),
+    "ps": ("psum", [128, 8 * BANK], "float32"),
+}
+SEMAPHORES = (["sw1", "sx", "srs", "sw2", "qw1", "qx", "qw2", "qh", "dd", "y0", "y1", "c0", "c1", "t0", "t1",
+               "rw", "rh", "lr", "wi1", "wi2", "wi3", "hi0", "hi1", "lc", "ld"]
+              + ["z%d" % p for p in range(NP)] + ["a%d" % p for p in range(NP)])
+
+
+def _bits(m):
+    return [e for e in range(m.bit_length()) if (m >> e) & 1]
+
+
+def _mask(engines):
+    m = 0
+    for e in engines:
+        m |= 1 << e
+    return m
+
+
+def _tr(src, cols, dsts, engines, rsem):
+    return {"src": src, "cols": cols, "dsts": dsts, "eng": engines, "rsem": rsem}
+
+
+def _split(engines, k):
+    n = len(engines) // k
+    return [engines[i * n:(i + 1) * n] for i in range(k)]
+
+
+def _plan(cores, topo):
+    calls, when = [], {}
+    for j, s in enumerate(cores):
+        dests = [(i, cores[(j - i) % N]) for i in range(1, G)]
+        straight = [x for x in dests if topo.may_write(s, x[1])]
+        relayed = [x for x in dests if not topo.may_write(s, x[1])]
+        able = [k for k in range(SIM) if k != s and topo.chip(k) == topo.chip(s) and topo.may_write(k, relayed[0][1])]
+        near = [k for k in able if topo.die(k) == topo.die(s)][:2]
+        far = [k for k in able if topo.die(k) != topo.die(s)][:2]
+        lo = _bits(topo.mask(s, dests[0][1]))
+        hi = [e for e in _bits(topo.mask(s, near[0])) if e not in lo]
+        for i, d in straight:
+            when[(d, i)] = 1
+        for n, (i, d) in enumerate(relayed):
+            when[(d, i)] = 2 + n
+        for own, land, inb, H, eng in (("w1q", "rwq", "wiq", near, hi), ("w1s", "rws", "wis", far, lo)):
+            if len(relayed) == 2:
+                trs = [_tr(own, (0, WC), [(H[0], land, (0, WC)), (H[1], land, (0, WC))], eng, "rw")]
+                jobs = [(H[0], (0, WC), relayed[0]), (H[1], (0, WC), relayed[1])]
+            else:
+                e2, m = _split(eng, 2), WC // 2
+                trs = [_tr(own, (0, m), [(H[0], land, (0, m))], e2[0], "rw"),
+                       _tr(own, (m, WC), [(H[1], land, (m, WC))], e2[1], "rw")]
+                jobs = [(H[0], (0, m), relayed[0]), (H[1], (m, WC), relayed[0])]
+            calls.append({"core": s, "wait": "qw1", "lsem": "lc", "trs": trs})
+            for h, (a, b), (i, d) in jobs:
+                o = (i - 1) * WC
+                calls.append({"core": h, "wait": "rw", "lsem": "lr",
+                              "trs": [_tr(land, (a, b), [(d, inb, (o + a, o + b))], _bits(topo.mask(h, d)), "wi%d" % i)]})
+        for own, inb in (("w1q", "wiq"), ("w1s", "wis")):
+            es = _split(lo, len(straight))
+            calls.append({"core": s, "wait": "qw1", "lsem": "ld",
+                          "trs": [_tr(own, (0, WC), [(d, inb, ((i - 1) * WC, i * WC))], es[n], "wi%d" % i)
+                                  for n, (i, d) in enumerate(straight)]})
+        d = cores[(j - 1) % N]
+        halves = [(0, HC), (HC, NC)]
+        for own, land, inb, H in (("hq", "rhq", "hiq", near), ("hs", "rhs", "his", far)):
+            if topo.may_write(s, d):
+                es = _split(lo, 2)
+                calls.append({"core": s, "wait": "qh", "lsem": "ld",
+                              "trs": [_tr(own, c, [(d, inb, c)], es[k], "hi%d" % k) for k, c in enumerate(halves)]})
+            else:
+                es = [lo, hi]
+                calls.append({"core": s, "wait": "qh", "lsem": "ld",
+                              "trs": [_tr(own, c, [(H[k], land, c)], es[k], "rh") for k, c in enumerate(halves)]})
+                for k, c in enumerate(halves):
+                    calls.append({"core": H[k], "wait": "rh", "lsem": "lr",
+                                  "trs": [_tr(land, c, [(d, inb, c)], _bits(topo.mask(H[k], d)), "hi%d" % k)]})
+    return calls, when
+
+
+def _lands(calls, core, sem):
+    return sum(len(t["eng"]) for c in calls for t in c["trs"] for x in t["dsts"] if x[0] == core and t["rsem"] == sem)
+
+
+def _view(T, buf, cols):
+    v = T[buf][:, cols[0]:cols[1]]
+    return v.bitcast(dt.uint8) if buf.endswith("q") else v
+
+
+def _issue(g, T, topo, call):
+    trs = []
+    for t in call["trs"]:
+        ids = []
+        for x in t["dsts"]:
+            rid, pid, _ = topo.addr(x[0])
+            ids.append(DstId(rid=rid, pnc=pid))
+        trs.append(RemoteDMATransfer(dst_ids=ids, dma_engine_mask=_mask(t["eng"]), remote_sem=T.sem[t["rsem"]],
+                                     srcs=[_view(T, t["src"], t["cols"])], dsts=[_view(T, x[1], x[2]) for x in t["dsts"]]))
+    g.remote_dma_fused(trs, local_sem=T.sem[call["lsem"]])
+    return sum(len(t["eng"]) for t in call["trs"])
+
+
+def _remote(g, core, T, topo, calls):
+    left, waited = {}, set()
+    for call in calls:
+        if call["core"] != core:
+            continue
+        w = call["wait"]
+        if w not in waited:
+            waited.add(w)
+            g.wait_ge(T.sem[w], 1 if w.startswith("q") else _lands(calls, core, w))
+        left[call["lsem"]] = left.get(call["lsem"], 0) + _issue(g, T, topo, call)
+    return left
+
+
+def rank_program(g, core, T, topo):
+    cores = list(T.cores)
+    calls, when = _plan(cores, topo)
+    S = T.sem
+    if T.rank_of(core) is None:
+        left = _remote(g, core, T, topo, calls)
+        for name in left:
+            g.wait_ge(S[name], left[name])
+        return
+
+    sy, sc, ve, te = g.sync, g.scalar, g.vector, g.tensor
+    order = sorted(range(G), key=lambda i: (when[(core, i)] if i else 0, i))
+    pieces, early = [], 0
+    for i in order:
+        if i == 0 or when[(core, i)] == 1:
+            pieces.append((i, 0, NC))
+            early += 1
+        else:
+            pieces += [(i, 0, HC), (i, HC, NC)]
+    ybank = [len(pieces), len(pieces) + 1]
+
+    left = _remote(g, core, T, topo, calls)
+    g.wait_ge(S.ld, left["ld"])
+
+    sy.dma_start(T.w1b[:], T.w1[:]).then_inc(S.sw1, 16)
+    sy.dma_start(T.xb[:], T.x[:]).then_inc(S.sx, 16)
+    sy.wait_ge(S.lc, left["lc"])
+    sy.dma_start(T.rsb[:], T.res[:]).then_inc(S.srs, 16)
+    sy.dma_start(T.w2b[:], T.w2[:]).then_inc(S.sw2, 16)
+    sy.wait_ge(S.c0, 1)
+    sy.dma_start(T.y[:, 0:HC], T.yb[:, 0:HC]).then_inc(S.t0, 16)
+    sy.wait_ge(S.t0, 16)
+
+    te.wait_ge(S.qw1, 1)
+    te.wait_ge(S.qx, 1)
+    seen = set()
+    for p, (i, a, b) in enumerate(pieces):
+        if i and i not in seen:
+            seen.add(i)
+            te.wait_ge(S["wi%d" % i], _lands(calls, core, "wi%d" % i))
+        lq, ls = (T.w1q[:], T.w1s[:]) if i == 0 else (T.wiq[:, (i - 1) * WC:i * WC], T.wis[:, (i - 1) * WC:i * WC])
+        te.matmul_mx(T.ps[:, p * BANK:p * BANK + b - a], lq, ls, T.xq[:, a:b], T.xs[:, a:b], True, True).then_inc(S["z%d" % p], 1)
+    te.wait_ge(S.qw2, 1)
+    te.wait_ge(S.qh, 1)
+    for k in range(2):
+        o = ybank[k] * BANK
+        te.matmul_mx(T.ps[:, o:o + HC], T.w2q[:, 0:WC], T.w2s[:, 0:WC],
+                     T.hq[:, k * HC:(k + 1) * HC], T.hs[:, k * HC:(k + 1) * HC], True, False)
+    for k in range(2):
+        o = ybank[k] * BANK
+        te.wait_ge(S["hi%d" % k], _lands(calls, core, "hi%d" % k))
+        te.matmul_mx(T.ps[:, o:o + HC], T.w2q[:, WC:2 * WC], T.w2s[:, WC:2 * WC],
+                     T.hiq[:, k * HC:(k + 1) * HC], T.his[:, k * HC:(k + 1) * HC], False, True).then_inc(S["y%d" % k], 1)
+
+    for p, (i, a, b) in enumerate(pieces):
+        sc.wait_ge(S["z%d" % p], 1)
+        sc.activation(T.ac[:, i * NC + a:i * NC + b], T.ps[:, p * BANK:p * BANK + b - a],
+                      ActivationFunctionType.Relu, scale=CF).then_inc(S["a%d" % p], 1)
+    sc.wait_ge(S.y1, 1)
+    sc.activation(T.yb[:, HC:NC], T.ps[:, ybank[1] * BANK:ybank[1] * BANK + HC], ActivationFunctionType.Copy).then_inc(S.c1, 1)
+    sc.wait_ge(S.c1, 1)
+    sc.dma_start(T.y[:, HC:NC], T.yb[:, HC:NC]).then_inc(S.t1, 16)
+    sc.wait_ge(S.t1, 16)
+
+    ve.wait_ge(S.sw1, 16)
+    ve.quantize_mx(T.w1q[:], T.w1s[:], T.w1b[:]).then_inc(S.qw1, 1)
+    ve.wait_ge(S.sx, 16)
+    ve.quantize_mx(T.xq[:], T.xs[:], T.xb[:]).then_inc(S.qx, 1)
+    ve.wait_ge(S.srs, 16)
+    for p, (i, a, b) in enumerate(pieces):
+        if p == early:
+            ve.wait_ge(S.sw2, 16)
+            ve.quantize_mx(T.w2q[:], T.w2s[:], T.w2b[:]).then_inc(S.qw2, 1)
+        ve.wait_ge(S["a%d" % p], 1)
+        ve.tensor_tensor(T.hb[:, 4 * a + i:4 * b:4], T.ac[:, i * NC + a:i * NC + b], T.rsb[:, 4 * a + i:4 * b:4],
+                         AluOpType.add).then_inc(S.dd, 1)
+    ve.wait_ge(S.dd, len(pieces))
+    ve.quantize_mx(T.hq[:], T.hs[:], T.hb[:]).then_inc(S.qh, 1)
+    ve.wait_ge(S.y0, 1)
+    ve.tensor_copy(T.yb[:, 0:HC], T.ps[:, ybank[0] * BANK:ybank[0] * BANK + HC]).then_inc(S.c0, 1)

@@ -26,7 +26,7 @@ SCRATCH = {
     "yb": ("sbuf", [128, NC], "float32"),
     "ps": ("psum", [128, 8 * BANK], "float32"),
 }
-SEMAPHORES = (["sw1", "sx", "srs", "sw2", "qw1", "qx", "qw2", "qh", "dd", "y0", "y1", "c0", "c1", "t0", "t1",
+SEMAPHORES = (["sw1", "sx", "srs", "sw2", "qw1", "qx", "qw2", "qh0", "qh1", "dd", "y0", "y1", "c0", "c1", "t0", "t1",
                "rw", "rh", "lr", "wi1", "wi2", "wi3", "hi0", "hi1", "lc", "ld"]
               + ["z%d" % p for p in range(NP)] + ["a%d" % p for p in range(NP)])
 
@@ -86,17 +86,12 @@ def _plan(cores, topo):
                           "trs": [_tr(own, (0, WC), [(d, inb, ((i - 1) * WC, i * WC))], es[n], "wi%d" % i)
                                   for n, (i, d) in enumerate(straight)]})
         d = cores[(j - 1) % N]
-        halves = [(0, HC), (HC, NC)]
-        for own, land, inb, H in (("hq", "rhq", "hiq", near), ("hs", "rhs", "his", far)):
-            if topo.may_write(s, d):
-                es = _split(lo, 2)
-                calls.append({"core": s, "wait": "qh", "lsem": "ld",
-                              "trs": [_tr(own, c, [(d, inb, c)], es[k], "hi%d" % k) for k, c in enumerate(halves)]})
-            else:
-                es = [lo, hi]
-                calls.append({"core": s, "wait": "qh", "lsem": "ld",
-                              "trs": [_tr(own, c, [(H[k], land, c)], es[k], "rh") for k, c in enumerate(halves)]})
-                for k, c in enumerate(halves):
+        for k, c in enumerate([(0, HC), (HC, NC)]):
+            for own, land, inb, H in (("hq", "rhq", "hiq", near), ("hs", "rhs", "his", far)):
+                if topo.may_write(s, d):
+                    calls.append({"core": s, "wait": "qh%d" % k, "lsem": "ld", "trs": [_tr(own, c, [(d, inb, c)], lo, "hi%d" % k)]})
+                else:
+                    calls.append({"core": s, "wait": "qh%d" % k, "lsem": "ld", "trs": [_tr(own, c, [(H[k], land, c)], lo + hi, "rh")]})
                     calls.append({"core": H[k], "wait": "rh", "lsem": "lr",
                                   "trs": [_tr(land, c, [(d, inb, c)], _bits(topo.mask(H[k], d)), "hi%d" % k)]})
     return calls, when
@@ -180,9 +175,9 @@ def rank_program(g, core, T, topo):
         lq, ls = (T.w1q[:], T.w1s[:]) if i == 0 else (T.wiq[:, (i - 1) * WC:i * WC], T.wis[:, (i - 1) * WC:i * WC])
         te.matmul_mx(T.ps[:, p * BANK:p * BANK + b - a], lq, ls, T.xq[:, a:b], T.xs[:, a:b], True, True).then_inc(S["z%d" % p], 1)
     te.wait_ge(S.qw2, 1)
-    te.wait_ge(S.qh, 1)
     for k in range(2):
         o = ybank[k] * BANK
+        te.wait_ge(S["qh%d" % k], 1)
         te.matmul_mx(T.ps[:, o:o + HC], T.w2q[:, 0:WC], T.w2s[:, 0:WC],
                      T.hq[:, k * HC:(k + 1) * HC], T.hs[:, k * HC:(k + 1) * HC], True, False)
     for k in range(2):
@@ -213,7 +208,9 @@ def rank_program(g, core, T, topo):
         ve.wait_ge(S["a%d" % p], 1)
         ve.tensor_tensor(T.hb[:, 4 * a + i:4 * b:4], T.ac[:, i * NC + a:i * NC + b], T.rsb[:, 4 * a + i:4 * b:4],
                          AluOpType.add).then_inc(S.dd, 1)
-    ve.wait_ge(S.dd, len(pieces))
-    ve.quantize_mx(T.hq[:], T.hs[:], T.hb[:]).then_inc(S.qh, 1)
+        k = p - (len(pieces) - 2)
+        if k >= 0:
+            ve.wait_ge(S.dd, p + 1)
+            ve.quantize_mx(T.hq[:, a:b], T.hs[:, a:b], T.hb[:, 4 * a:4 * b]).then_inc(S["qh%d" % k], 1)
     ve.wait_ge(S.y0, 1)
     ve.tensor_copy(T.yb[:, 0:HC], T.ps[:, ybank[0] * BANK:ybank[0] * BANK + HC]).then_inc(S.c0, 1)

from concourse.bass import DstId, RemoteDMATransfer
from concourse.mybir import dt, AluOpType, ActivationFunctionType

N = 9
SIM = 96
NC = 512
WC = 128
G = 4
HC = NC // 2
CF = 0.047
BANK = 512
NP = 6

_Q, _U = "float8_e4m3fn_x4", "uint8"
SCRATCH = {
    "w1b": ("sbuf", [128, 4 * WC], "bfloat16"), "w1q": ("sbuf", [128, WC], _Q), "w1s": ("sbuf", [128, WC], _U),
    "xb": ("sbuf", [128, 4 * NC], "bfloat16"), "xq": ("sbuf", [128, NC], _Q), "xs": ("sbuf", [128, NC], _U),
    "w2b": ("sbuf", [128, 8 * WC], "bfloat16"), "w2q": ("sbuf", [128, 2 * WC], _Q), "w2s": ("sbuf", [128, 2 * WC], _U),
    "rsb": ("sbuf", [128, 4 * NC], "bfloat16"),
    "ac": ("sbuf", [128, G * NC], "float32"),
    "hb": ("sbuf", [128, 4 * NC], "bfloat16"), "hq": ("sbuf", [128, NC], _Q), "hs": ("sbuf", [128, NC], _U),
    "wiq": ("sbuf", [128, 3 * WC], _Q), "wis": ("sbuf", [128, 3 * WC], _U),
    "hiq": ("sbuf", [128, NC], _Q), "his": ("sbuf", [128, NC], _U),
    "rwq": ("sbuf", [128, WC], _Q), "rws": ("sbuf", [128, WC], _U),
    "rhq": ("sbuf", [128, NC], _Q), "rhs": ("sbuf", [128, NC], _U),
    "yb": ("sbuf", [128, NC], "float32"),
    "ps": ("psum", [128, 8 * BANK], "float32"),
}
SEMAPHORES = (["sw1", "sx", "srs", "sw2", "qw1", "qx", "qw2", "qh0", "qh1", "dd", "y0", "y1", "c0", "c1", "t0", "t1",
               "rw", "rh", "lr", "wi1", "wi2", "wi3", "hi0", "hi1", "lc", "ld"]
              + ["z%d" % p for p in range(NP)] + ["a%d" % p for p in range(NP)])


def _bits(m):
    return [e for e in range(m.bit_length()) if (m >> e) & 1]


def _mask(engines):
    m = 0
    for e in engines:
        m |= 1 << e
    return m


def _tr(src, cols, dsts, engines, rsem):
    return {"src": src, "cols": cols, "dsts": dsts, "eng": engines, "rsem": rsem}


def _split(engines, k):
    n = len(engines) // k
    return [engines[i * n:(i + 1) * n] for i in range(k)]


def _plan(cores, topo):
    calls, when = [], {}
    for j, s in enumerate(cores):
        dests = [(i, cores[(j - i) % N]) for i in range(1, G)]
        straight = [x for x in dests if topo.may_write(s, x[1])]
        relayed = [x for x in dests if not topo.may_write(s, x[1])]
        able = [k for k in range(SIM) if k != s and topo.chip(k) == topo.chip(s) and topo.may_write(k, relayed[0][1])]
        near = [k for k in able if topo.die(k) == topo.die(s)][:2]
        far = [k for k in able if topo.die(k) != topo.die(s)][:2]
        lo = _bits(topo.mask(s, dests[0][1]))
        hi = [e for e in _bits(topo.mask(s, near[0])) if e not in lo]
        for i, d in straight:
            when[(d, i)] = 1
        for n, (i, d) in enumerate(relayed):
            when[(d, i)] = 2 + n
        for own, land, inb, H, eng in (("w1q", "rwq", "wiq", near, hi), ("w1s", "rws", "wis", far, lo)):
            if len(relayed) == 2:
                trs = [_tr(own, (0, WC), [(H[0], land, (0, WC)), (H[1], land, (0, WC))], eng, "rw")]
                jobs = [(H[0], (0, WC), relayed[0]), (H[1], (0, WC), relayed[1])]
            else:
                e2, m = _split(eng, 2), WC // 2
                trs = [_tr(own, (0, m), [(H[0], land, (0, m))], e2[0], "rw"),
                       _tr(own, (m, WC), [(H[1], land, (m, WC))], e2[1], "rw")]
                jobs = [(H[0], (0, m), relayed[0]), (H[1], (m, WC), relayed[0])]
            calls.append({"core": s, "wait": "qw1", "lsem": "lc", "trs": trs})
            for h, (a, b), (i, d) in jobs:
                o = (i - 1) * WC
                calls.append({"core": h, "wait": "rw", "lsem": "lr",
                              "trs": [_tr(land, (a, b), [(d, inb, (o + a, o + b))], _bits(topo.mask(h, d)), "wi%d" % i)]})
        for own, inb in (("w1q", "wiq"), ("w1s", "wis")):
            es = _split(lo, len(straight))
            calls.append({"core": s, "wait": "qw1", "lsem": "ld",
                          "trs": [_tr(own, (0, WC), [(d, inb, ((i - 1) * WC, i * WC))], es[n], "wi%d" % i)
                                  for n, (i, d) in enumerate(straight)]})
        d = cores[(j - 1) % N]
        for k, c in enumerate([(0, HC), (HC, NC)]):
            for own, land, inb, H in (("hq", "rhq", "hiq", near), ("hs", "rhs", "his", far)):
                if topo.may_write(s, d):
                    calls.append({"core": s, "wait": "qh%d" % k, "lsem": "ld", "trs": [_tr(own, c, [(d, inb, c)], lo, "hi%d" % k)]})
                else:
                    calls.append({"core": s, "wait": "qh%d" % k, "lsem": "ld", "trs": [_tr(own, c, [(H[k], land, c)], lo + hi, "rh")]})
                    calls.append({"core": H[k], "wait": "rh", "lsem": "lr",
                                  "trs": [_tr(land, c, [(d, inb, c)], _bits(topo.mask(H[k], d)), "hi%d" % k)]})
    return calls, when


def _lands(calls, core, sem):
    return sum(len(t["eng"]) for c in calls for t in c["trs"] for x in t["dsts"] if x[0] == core and t["rsem"] == sem)


def _view(T, buf, cols):
    v = T[buf][:, cols[0]:cols[1]]
    return v.bitcast(dt.uint8) if buf.endswith("q") else v


def _issue(g, T, topo, call):
    trs = []
    for t in call["trs"]:
        ids = []
        for x in t["dsts"]:
            rid, pid, _ = topo.addr(x[0])
            ids.append(DstId(rid=rid, pnc=pid))
        trs.append(RemoteDMATransfer(dst_ids=ids, dma_engine_mask=_mask(t["eng"]), remote_sem=T.sem[t["rsem"]],
                                     srcs=[_view(T, t["src"], t["cols"])], dsts=[_view(T, x[1], x[2]) for x in t["dsts"]]))
    g.remote_dma_fused(trs, local_sem=T.sem[call["lsem"]])
    return sum(len(t["eng"]) for t in call["trs"])


def _remote(g, core, T, topo, calls):
    left, waited = {}, set()
    for call in calls:
        if call["core"] != core:
            continue
        w = call["wait"]
        if w not in waited:
            waited.add(w)
            g.wait_ge(T.sem[w], 1 if w.startswith("q") else _lands(calls, core, w))
        left[call["lsem"]] = left.get(call["lsem"], 0) + _issue(g, T, topo, call)
    return left


def rank_program(g, core, T, topo):
    cores = list(T.cores)
    calls, when = _plan(cores, topo)
    S = T.sem
    if T.rank_of(core) is None:
        left = _remote(g, core, T, topo, calls)
        for name in left:
            g.wait_ge(S[name], left[name])
        return

    sy, sc, ve, te = g.sync, g.scalar, g.vector, g.tensor
    order = sorted(range(G), key=lambda i: (when[(core, i)] if i else 0, i))
    pieces, early = [], 0
    for i in order:
        if i == 0 or when[(core, i)] == 1:
            pieces.append((i, 0, NC))
            early += 1
        else:
            pieces += [(i, 0, HC), (i, HC, NC)]
    ybank = [len(pieces), len(pieces) + 1]

    left = _remote(g, core, T, topo, calls)
    g.wait_ge(S.ld, left["ld"])

    sy.dma_start(T.w1b[:], T.w1[:]).then_inc(S.sw1, 16)
    sy.dma_start(T.xb[:], T.x[:]).then_inc(S.sx, 16)
    sy.wait_ge(S.lc, left["lc"])
    sy.dma_start(T.rsb[:], T.res[:]).then_inc(S.srs, 16)
    sy.dma_start(T.w2b[:], T.w2[:]).then_inc(S.sw2, 16)
    sy.wait_ge(S.c0, 1)
    sy.dma_start(T.y[:, 0:HC], T.yb[:, 0:HC]).then_inc(S.t0, 16)
    sy.wait_ge(S.t0, 16)

    te.wait_ge(S.qw1, 1)
    te.wait_ge(S.qx, 1)
    seen = set()
    for p, (i, a, b) in enumerate(pieces):
        if i and i not in seen:
            seen.add(i)
            te.wait_ge(S["wi%d" % i], _lands(calls, core, "wi%d" % i))
        lq, ls = (T.w1q[:], T.w1s[:]) if i == 0 else (T.wiq[:, (i - 1) * WC:i * WC], T.wis[:, (i - 1) * WC:i * WC])
        te.matmul_mx(T.ps[:, p * BANK:p * BANK + b - a], lq, ls, T.xq[:, a:b], T.xs[:, a:b], True, True).then_inc(S["z%d" % p], 1)
    te.wait_ge(S.qw2, 1)
    for k in range(2):
        o = ybank[k] * BANK
        te.wait_ge(S["qh%d" % k], 1)
        te.matmul_mx(T.ps[:, o:o + HC], T.w2q[:, 0:WC], T.w2s[:, 0:WC],
                     T.hq[:, k * HC:(k + 1) * HC], T.hs[:, k * HC:(k + 1) * HC], True, False)
    for k in range(2):
        o = ybank[k] * BANK
        te.wait_ge(S["hi%d" % k], _lands(calls, core, "hi%d" % k))
        te.matmul_mx(T.ps[:, o:o + HC], T.w2q[:, WC:2 * WC], T.w2s[:, WC:2 * WC],
                     T.hiq[:, k * HC:(k + 1) * HC], T.his[:, k * HC:(k + 1) * HC], False, True).then_inc(S["y%d" % k], 1)

    for p, (i, a, b) in enumerate(pieces):
        sc.wait_ge(S["z%d" % p], 1)
        sc.activation(T.ac[:, i * NC + a:i * NC + b], T.ps[:, p * BANK:p * BANK + b - a],
                      ActivationFunctionType.Relu, scale=CF).then_inc(S["a%d" % p], 1)
    sc.wait_ge(S.y1, 1)
    sc.activation(T.yb[:, HC:NC], T.ps[:, ybank[1] * BANK:ybank[1] * BANK + HC], ActivationFunctionType.Copy).then_inc(S.c1, 1)
    sc.wait_ge(S.c1, 1)
    sc.dma_start(T.y[:, HC:NC], T.yb[:, HC:NC]).then_inc(S.t1, 16)
    sc.wait_ge(S.t1, 16)

    ve.wait_ge(S.sw1, 16)
    ve.quantize_mx(T.w1q[:], T.w1s[:], T.w1b[:]).then_inc(S.qw1, 1)
    ve.wait_ge(S.sx, 16)
    ve.quantize_mx(T.xq[:], T.xs[:], T.xb[:]).then_inc(S.qx, 1)
    ve.wait_ge(S.srs, 16)
    for p, (i, a, b) in enumerate(pieces):
        if p == early:
            ve.wait_ge(S.sw2, 16)
            ve.quantize_mx(T.w2q[:], T.w2s[:], T.w2b[:]).then_inc(S.qw2, 1)
        ve.wait_ge(S["a%d" % p], 1)
        ve.tensor_tensor(T.hb[:, 4 * a + i:4 * b:4], T.ac[:, i * NC + a:i * NC + b], T.rsb[:, 4 * a + i:4 * b:4],
                         AluOpType.add).then_inc(S.dd, 1)
        k = p - (len(pieces) - 2)
        if k >= 0:
            ve.wait_ge(S.dd, p + 1)
            ve.quantize_mx(T.hq[:, a:b], T.hs[:, a:b], T.hb[:, 4 * a:4 * b]).then_inc(S["qh%d" % k], 1)
    ve.wait_ge(S.y0, 1)
    ve.tensor_copy(T.yb[:, 0:HC], T.ps[:, ybank[0] * BANK:ybank[0] * BANK + HC]).then_inc(S.c0, 1)
